import numpy as np
import ml_dtypes


def mxq(x, axis, fmt="e4m3"):
    dtype, down = {"e4m3": (ml_dtypes.float8_e4m3fn, 7), "e5m2": (ml_dtypes.float8_e5m2, 14)}[fmt]
    v = np.moveaxis(np.asarray(x, np.float32).astype(ml_dtypes.bfloat16).astype(np.float64), axis, -1)
    blocks = v.reshape(v.shape[:-1] + (-1, 32))
    amax = np.abs(blocks).max(-1, keepdims=True)
    byte = np.maximum(np.where(amax > 0, np.frexp(amax)[1] - 1 + 127, 0) - down, 1)
    scale = np.exp2(byte - 127.0)
    codes = (blocks / scale).astype(np.float32).astype(dtype).astype(np.float64)
    return np.moveaxis((codes * scale).reshape(v.shape), -1, axis)


WIDE = False


def mx_kscale(k):
    if not WIDE:
        return np.ones(k)
    levels = np.array([10, -10, 5, -5, 0])
    if k % 512:
        return np.exp2(np.random.permutation(np.resize(levels, k // 32))).repeat(32)
    a = np.empty((k // 512, 16))
    for p in range(k // 512):
        a[p, :8] = np.random.permutation(np.resize(levels, 8))
        for g in range(8):
            far = levels[np.abs(levels - a[p, g]) >= 10]
            a[p, g + 8] = far[np.random.randint(len(far))]
    return np.exp2(a.ravel()).repeat(32)


BF16 = ml_dtypes.bfloat16


def bf(x):
    return np.asarray(x, np.float32).astype(BF16)


def f64(x):
    return np.asarray(x).astype(np.float64)


E2M1 = np.array([0.0, 0.5, 1.0, 1.5, 2.0, 3.0, 4.0, 6.0, -0.0, -0.5, -1.0, -1.5, -2.0, -3.0, -4.0, -6.0])


def pack_weight(w, fmt):
    k, n = w.shape
    w = f64(bf(w)).reshape(k // 32, 32, n)
    amax = np.abs(w).max(1)
    if fmt == "e4m3":
        byte = np.frexp(amax)[1] - 1 + 127 - 7
    else:
        mant, ex = np.frexp(amax / 6.0)
        byte = np.where(mant > 0.5, ex, ex - 1) + 127
    byte = np.clip(np.where(amax > 0, byte, 1), 1, 254)
    scaled = (w * np.exp2(127.0 - byte)[:, None, :]).reshape(k, n).astype(np.float32)
    by_word = np.ascontiguousarray(scaled.reshape(k // 512, 128, 4, n).transpose(0, 1, 3, 2))
    if fmt == "e4m3":
        words = by_word.astype(ml_dtypes.float8_e4m3fn).view(np.uint8)
    else:
        c = by_word.astype(ml_dtypes.float4_e2m1fn).view(np.uint8) & 0xF
        words = c[..., 0::2] | (c[..., 1::2] << 4)
    return np.ascontiguousarray(words), np.ascontiguousarray(byte.astype(np.uint8).reshape(k // 512, 16, n))


def unpack_weight(words, scales, fmt):
    g, p, n, _ = words.shape
    if fmt == "e4m3":
        vals = np.ascontiguousarray(words).view(ml_dtypes.float8_e4m3fn).astype(np.float64)
    else:
        nib = np.empty((g, p, n, 4), np.uint8)
        nib[..., 0::2] = words & 0xF
        nib[..., 1::2] = words >> 4
        vals = E2M1[nib]
    vals = vals * np.repeat(np.exp2(scales.astype(np.float64) - 127.0), 8, axis=1)[..., None]
    return vals.transpose(0, 1, 3, 2).reshape(g * 512, n)
def pack4(w):
    words, scales = pack_weight(w, "e2m1")
    return words.reshape(words.shape[0], 128, -1), scales


def unpack4(words, scales):
    return unpack_weight(words.reshape(words.shape[0], 128, -1, 2), scales, "e2m1")


E4M3FN = np.array([(-1.0 if i & 128 else 1.0) * ((1.0 + (i & 7) / 8.0) * 2.0 ** (((i >> 3) & 15) - 7) if i & 120 else (i & 7) * 2.0 ** -9) for i in range(256)])


def e4m3fn_bytes(y):
    return np.clip(np.asarray(y, np.float64), -448.0, 448.0).astype(np.float32).astype(ml_dtypes.float8_e4m3fn).view(np.uint8)


def e4m3fn_values(b):
    return E4M3FN[b]


N, D, C, H = 1024, 512, 512, 1024
G = 2 * D
EPS = 1e-5


def elu(v):
    return np.where(v > 0.0, v, np.exp(np.minimum(v, 0.0)) - 1.0)


def sigmoid(v):
    return 1.0 / (1.0 + np.exp(-v))


def normalize_rows(r):
    mean = np.mean(r, axis=-1, keepdims=True)
    centered = r - mean
    var = np.mean(centered * centered, axis=-1, keepdims=True)
    return centered / np.sqrt(var + EPS)


def draw0():
    sa, sc, t = mx_kscale(D), mx_kscale(C), mx_kscale(H)
    row_scale = np.exp(0.3 * np.random.standard_normal((N, 1)))
    row_offset = 0.3 * np.random.standard_normal((N, 1))
    a = np.random.standard_normal((N, D)) * row_scale + row_offset
    c = np.random.standard_normal((N, C))
    wa = np.random.standard_normal((D, H)) / np.sqrt(D)
    wc = np.random.standard_normal((C, H)) / np.sqrt(C)
    gain = 1.0 + 0.1 * np.random.standard_normal(H)
    wgv = np.random.standard_normal((H, G)) / np.sqrt(H)
    skip = 1.0 + 0.1 * np.random.standard_normal(D)
    wa_words, wa_scales = pack4(wa / sa[:, None])
    wc_words, wc_scales = pack4(wc / sc[:, None])
    wgv_words, wgv_scales = pack4(wgv / t[:, None])
    return {
        "a": bf(a * sa),
        "c": bf(c * sc),
        "wa_words": wa_words,
        "wa_scales": wa_scales,
        "wc_words": wc_words,
        "wc_scales": wc_scales,
        "gain": bf(gain * t),
        "wgv_words": wgv_words,
        "wgv_scales": wgv_scales,
        "skip": bf(skip / sa),
    }


def core(a, c, wa_words, wa_scales, wc_words, wc_scales, gain, wgv_words, wgv_scales, skip):
    a, c = f64(a), f64(c)
    wa = unpack4(wa_words, wa_scales)
    wc = unpack4(wc_words, wc_scales)
    wgv = unpack4(wgv_words, wgv_scales)
    gain, skip = f64(gain), f64(skip)
    d = a.shape[-1]
    t = (mxq(a, 1, "e4m3") @ wa) + (mxq(c, 1, "e4m3") @ wc)
    m = gain[None, :] * elu(t)
    z = mxq(m, 1, "e4m3") @ wgv
    u = sigmoid(z[:, :d]) * z[:, d:]
    r = skip[None, :] * a + u
    return normalize_rows(r)


def setup_inputs():
    drawn = draw0()
    full = np.asarray(drawn['c']).astype(np.float64)
    scale = (np.abs(full).reshape(1024, 4, 128).max(axis=(2,)) / 448.0).astype(np.float32)
    given = {}
    for key, value in drawn.items():
        if key == 'c':
            given['c_bytes'] = e4m3fn_bytes(full / np.repeat(scale.astype(np.float64), 128, axis=1))
            given['c_scale'] = scale
        else:
            given[key] = value
    return given


def reference(a, c_bytes, c_scale, wa_words, wa_scales, wc_words, wc_scales, gain, wgv_words, wgv_scales, skip):
    return core(a, e4m3fn_values(c_bytes) * np.repeat(c_scale.astype(np.float64), 128, axis=1), wa_words, wa_scales, wc_words, wc_scales, gain, wgv_words, wgv_scales, skip)

@@ -1,0 +1,475 @@
+from contextlib import ExitStack
+
+import concourse.mybir as mybir
+from concourse.masks import make_identity
+
+N, D, H = 1024, 512, 1024
+EPS = 1e-5
+FLOPS = 2 * N * D * H * 2 + 2 * N * H * 2 * D
+
+F32 = mybir.dt.float32
+BF16 = mybir.dt.bfloat16
+I32 = mybir.dt.int32
+U32 = mybir.dt.uint32
+U8 = mybir.dt.uint8
+F8 = mybir.dt.float8_e4m3fn
+FP8X4 = mybir.dt.float8_e4m3fn_x4
+FP4X4 = mybir.dt.float4_e2m1fn_x4
+ALU = mybir.AluOpType
+ACT = mybir.ActivationFunctionType
+
+P = 128
+TILES = N // P
+MINUS_ON_VECTOR = [(0, 0), (1, 1), (2, 1)]
+DEQ_ON_VECTOR = [(4, 0), (4, 1), (4, 2), (4, 3), (5, 0), (5, 1), (5, 2), (5, 3)]
+NORM_ON_SCALAR = [0, 1, 2, 3, 4]
+
+
+def ZBANK(i, h):
+    return "z%d" % h if i < 7 else "t0%d" % h
+
+
+def tile_temporalfusioncontextgatedresidual_d1p_kernel(
+    tc, a, c_bytes, c_scale, wa_words, wa_scales, wc_words, wc_scales, gain, wgv_words, wgv_scales, skip, out
+):
+    nc = tc.nc
+    with ExitStack() as ctx:
+        keep = ctx.enter_context(tc.tile_pool(name="keep", bufs=1))
+        work = ctx.enter_context(tc.tile_pool(name="work", bufs=2))
+        psum = ctx.enter_context(tc.psum_pool(name="psum", bufs=1))
+        ctx.enter_context(tc.manual_schedule())
+
+        a_rows = a.rearrange("(p i) k -> p i k", i=TILES)
+        c_rows = c_bytes.rearrange("(p i) k -> p i k", i=TILES)
+        out_rows = out.rearrange("(p i) d -> p i d", i=TILES)
+
+        c_sc = keep.tile([P, TILES * 4], F32, name="c_sc")
+        w_raw = keep.tile([P, 2, 2 * H], U8, name="w_raw", align_bytes=64)
+        w_perm = keep.tile([P, 2, 8, 2 * P], U8, name="w_perm", align_bytes=64)
+        s_raw = keep.tile([P, 2, H], U8, name="s_raw", align_bytes=64)
+        s_perm = keep.tile([P, 2, 8, P], U8, name="s_perm", align_bytes=64)
+        g_words = keep.tile([P, 2, 2 * H], U8, name="g_words", align_bytes=64)
+        g_scales = keep.tile([P, 2, H], U8, name="g_scales", align_bytes=64)
+        gain_sb = keep.tile([P, 2, 4], BF16, name="gain_sb")
+        skip_sb = keep.tile([P, 4], BF16, name="skip_sb")
+        ident = keep.tile([P, P], F32, name="ident")
+        diag = keep.tile([P, 4, P], BF16, name="diag")
+        zero = keep.tile([P, 1], F32, name="zero")
+        minus = keep.tile([P, 1], F32, name="minus")
+        warm = keep.tile([P, 1], F32, name="warm")
+        neg_half = keep.tile([P, 1], F32, name="neg_half")
+
+        chunks = [(0, 2), (2, 4), (4, 8)]
+        a_sb, cb_sb = {}, {}
+        for lo, hi in chunks:
+            a_chunk = keep.tile([P, hi - lo, D], BF16, name="a_chunk%d" % lo)
+            cb_chunk = keep.tile([P, hi - lo, D], U8, name="cb_chunk%d" % lo)
+            for i in range(lo, hi):
+                a_sb[i] = a_chunk[:, i - lo, :]
+                cb_sb[i] = cb_chunk[:, i - lo, :]
+            a_sb["c%d" % lo] = a_chunk
+            cb_sb["c%d" % lo] = cb_chunk
+
+        def load_a(lo, hi):
+            nc.sync.dma_start(out=a_sb["c%d" % lo][:], in_=a_rows[:, lo:hi, :])
+
+        def load_c(lo, hi):
+            nc.sync.dma_start(out=cb_sb["c%d" % lo][:], in_=c_rows[:, lo:hi, :])
+
+        nc.vector.memset(zero[:], 0.0)
+        nc.vector.memset(s_raw[:].rearrange("p w n -> p (w n)").bitcast(I32), 0)
+        nc.vector.memset(g_scales[:].rearrange("p w n -> p (w n)").bitcast(I32), 0)
+        nc.vector.memset(neg_half[:], -0.5)
+        nc.vector.memset(minus[:], -1.0)
+
+        nc.sync.dma_start(out=w_raw[:, 0, :].bitcast(I32), in_=wa_words[0].bitcast(I32))
+        nc.sync.dma_start(out=w_raw[:, 1, :].bitcast(I32), in_=wc_words[0].bitcast(I32))
+        nc.sync.dma_start(out=c_sc[:], in_=c_scale.rearrange("(p i) q -> p (i q)", i=TILES))
+        load_c(*chunks[0])
+        load_a(*chunks[0])
+        make_identity(nc, ident[:])
+        for w, scales in ((1, wc_scales), (0, wa_scales)):
+            for q in range(4):
+                (nc.sync, nc.scalar)[w].dma_start(
+                    out=s_raw[32 * q : 32 * q + 4, w, :].bitcast(I32), in_=scales[0, 4 * q : 4 * q + 4, :].bitcast(I32)
+                )
+        nc.scalar.activation(out=warm[:], in_=zero[:], func=ACT.Exp)
+        load_c(*chunks[1])
+        load_a(*chunks[1])
+        nc.sync.dma_start(out=skip_sb[:], in_=skip.rearrange("(p t) -> p t", t=4))
+        nc.sync.dma_start(out=gain_sb[:], in_=gain.rearrange("(g p t) -> p g t", g=2, t=4))
+        load_c(*chunks[2])
+        load_a(*chunks[2])
+        for q in range(4):
+            nc.sync.dma_start(
+                out=g_scales[32 * q : 32 * q + 4, :, :].bitcast(I32),
+                in_=wgv_scales[:, 4 * q : 4 * q + 4, :].rearrange("g q n -> q g n").bitcast(I32),
+            )
+        for g in range(2):
+            nc.sync.dma_start(out=g_words[:, g, :].bitcast(I32), in_=wgv_words[g].bitcast(I32))
+
+        for t in range(4):
+            nc.gpsimd.tensor_scalar(
+                out=diag[:, t, :], in0=ident[:], scalar1=skip_sb[:, t : t + 1], scalar2=0.0, op0=ALU.mult, op1=ALU.add
+            )
+
+        def permute_words(w, g):
+            nc.vector.tensor_copy(
+                out=w_perm[:, w, 4 * g : 4 * g + 4, :].rearrange("p t (m b) -> p t m b", b=2),
+                in_=w_raw[:, w, H * g : H * (g + 1)].rearrange("p (m t b) -> p t m b", t=4, b=2),
+            )
+
+        def permute_scales(g):
+            nc.vector.tensor_copy(
+                out=s_perm[:, :, 4 * g : 4 * g + 4, :],
+                in_=s_raw[:, :, D * g : D * (g + 1)].rearrange("p w (m t) -> p w t m", t=4),
+            )
+
+        cw, tr, grp, xc, xs, tb, e, n, elu, mb, mc, ms = ({} for x in range(12))
+        zb, sa, th, u2, r, rsum, nm, ss, rstd, nb = ({} for x in range(10))
+
+        def dequant(i):
+            cw[i] = work.tile([P, D], BF16, name="cw", bufs=8)
+            for b in range(4):
+                blk = slice(P * b, P * (b + 1))
+                scale = c_sc[:, 4 * i + b : 4 * i + b + 1]
+                if (i, b) in DEQ_ON_VECTOR:
+                    nc.vector.tensor_scalar(out=cw[i][:, blk], in0=cb_sb[i][:, blk].bitcast(F8), scalar1=scale, scalar2=None, op0=ALU.mult)
+                else:
+                    nc.scalar.activation(out=cw[i][:, blk], in_=cb_sb[i][:, blk].bitcast(F8), func=ACT.Copy, scale=scale)
+
+        def turn(i):
+            tr[i] = psum.tile([P, 4, P], F32, name="tr")
+            for s, rows in enumerate((a_sb[i], cw[i][:])):
+                words = rows.bitcast(F32)
+                for u in range(2):
+                    nc.tensor.transpose(tr[i][:, 2 * s + u, :], words[:, u::2], ident[:])
+
+        def copy_out(i):
+            grp[i] = work.tile([P, 2 * D], BF16, name="grp", bufs=8, align_bytes=64)
+            nc.scalar.copy(
+                out=grp[i][:].bitcast(F32).rearrange("p (o r u) -> p o r u", o=2, u=2),
+                in_=tr[i][:].rearrange("p (o u) r -> p o r u", o=2),
+            )
+
+        def quant_in(i):
+            xc[i] = work.tile([P, 2 * P], U32, name="xc", bufs=8, align_bytes=64)
+            xs[i] = work.tile([P, 2 * P], U8, name="xs", bufs=8, align_bytes=64)
+            nc.vector.quantize_mx(out=xc[i][:].bitcast(FP8X4), scales=xs[i][:], in_=grp[i][:])
+
+        def first_matmuls(i, g):
+            if True:
+                tb[i, g] = psum.tile([P, 4 * P], F32, name="t%d%d" % (i % 2, g))
+                for t in range(4):
+                    for w in range(2):
+                        nc.tensor.matmul_mx(
+                            out=tb[i, g][:, P * t : P * (t + 1)],
+                            lhsT=w_perm[:, w, 4 * g + t, :].bitcast(FP4X4),
+                            lhsT_scale=s_perm[:, w, 4 * g + t, :],
+                            rhs=xc[i][:, P * w : P * (w + 1)].bitcast(FP8X4),
+                            rhs_scale=xs[i][:, P * w : P * (w + 1)],
+                            start=(w == 0),
+                            stop=(w == 1),
+                        )
+
+        def exps(i, g):
+            e[i, g] = work.tile([P, P, 4], F32, name="e%d" % g, bufs=3)
+            nc.scalar.activation(out=e[i, g][:], in_=tb[i, g][:].rearrange("p (t n) -> p n t", t=4), func=ACT.Exp)
+
+        def minus_one(i, g):
+            n[i, g] = work.tile([P, P, 4], F32, name="n%d" % g, bufs=4)
+            if (i, g) in MINUS_ON_VECTOR:
+                nc.vector.tensor_scalar(
+                    out=n[i, g][:].rearrange("p n t -> p (n t)"),
+                    in0=e[i, g][:].rearrange("p n t -> p (n t)"),
+                    scalar1=1.0,
+                    scalar2=None,
+                    op0=ALU.subtract,
+                )
+            else:
+                nc.scalar.activation(out=n[i, g][:], in_=e[i, g][:], func=ACT.Identity, bias=minus[:])
+
+        def elu_pass(i, g):
+            if i not in elu:
+                elu[i] = work.tile([P, 2, P, 4], F32, name="elu", bufs=3)
+            nc.vector.scalar_tensor_tensor(
+                out=elu[i][:, g, :, :],
+                in0=tb[i, g][:].rearrange("p (t n) -> p n t", t=4),
+                scalar=0.0,
+                in1=n[i, g][:],
+                op0=ALU.max,
+                op1=ALU.min,
+            )
+
+        def gain_pass(i):
+            mb[i] = work.tile([P, 2, P, 4], BF16, name="mb", bufs=3, align_bytes=64)
+            nc.vector.tensor_tensor(
+                out=mb[i][:], in0=elu[i][:], in1=gain_sb[:].unsqueeze(2).to_broadcast([P, 2, P, 4]), op=ALU.mult
+            )
+
+        def quant_m(i):
+            mc[i] = work.tile([P, 2 * P], U32, name="mc", bufs=3, align_bytes=64)
+            ms[i] = work.tile([P, 2 * P], U8, name="ms", bufs=3, align_bytes=64)
+            nc.vector.quantize_mx(
+                out=mc[i][:].bitcast(FP8X4), scales=ms[i][:], in_=mb[i][:].rearrange("p g n t -> p (g n t)")
+            )
+
+        def second_matmuls(i, h):
+            if True:
+                zb[i, h] = psum.tile([P, D], F32, name=ZBANK(i, h))
+                for g in range(2):
+                    nc.tensor.matmul_mx(
+                        out=zb[i, h][:],
+                        lhsT=mc[i][:, P * g : P * (g + 1)].bitcast(FP8X4),
+                        lhsT_scale=ms[i][:, P * g : P * (g + 1)],
+                        rhs=g_words[:, g, 2 * D * h : 2 * D * (h + 1)].bitcast(FP4X4),
+                        rhs_scale=g_scales[:, g, D * h : D * (h + 1)],
+                        start=(g == 0),
+                        stop=(g == 1),
+                    )
+
+        def skip_matmuls(i):
+            sa[i] = psum.tile([P, D], F32, name="sa" if i < 7 else "tr")
+            a_t = grp[i][:, 0:D].rearrange("p (r t) -> p t r", t=4)
+            for t in range(4):
+                nc.tensor.matmul(sa[i][:, P * t : P * (t + 1)], lhsT=a_t[:, t, :], rhs=diag[:, t, :], start=True, stop=True)
+
+        def gate_tanh(i):
+            th[i] = work.tile([P, D], F32, name="th", bufs=3)
+            nc.scalar.activation(out=th[i][:], in_=zb[i, 0][:], func=ACT.Tanh, scale=0.5)
+
+        def gate_pass(i):
+            u2[i] = work.tile([P, P, 4], F32, name="u2", bufs=3)
+            nc.vector.scalar_tensor_tensor(
+                out=u2[i][:].rearrange("p m t -> p (m t)"), in0=th[i][:], scalar=1.0, in1=zb[i, 1][:], op0=ALU.add, op1=ALU.mult
+            )
+
+        def residual_pass(i):
+            r[i] = work.tile([P, P, 4], F32, name="r", bufs=8)
+            rsum[i] = work.tile([P, 1], F32, name="rsum", bufs=8)
+            nc.vector.scalar_tensor_tensor(
+                out=r[i][:],
+                in0=u2[i][:],
+                scalar=0.5,
+                in1=sa[i][:].rearrange("p (t m) -> p m t", t=4),
+                op0=ALU.mult,
+                op1=ALU.add,
+                accum_out=rsum[i][:],
+            )
+
+        def squares(i):
+            nm[i] = work.tile([P, 1], F32, name="nm", bufs=8)
+            ss[i] = work.tile([P, 1], F32, name="ss", bufs=8)
+            sq = work.tile([P, D], F32, name="sq", bufs=2)
+            nc.scalar.mul(nm[i][:], rsum[i][:], -1.0 / D)
+            nc.scalar.activation(
+                out=sq[:], in_=r[i][:].rearrange("p m t -> p (m t)"), func=ACT.Square, bias=nm[i][:], accum_out=ss[i][:]
+            )
+
+        def scale_up(i):
+            rstd[i] = work.tile([P, 1], F32, name="rstd", bufs=8)
+            var = work.tile([P, 1], F32, name="var", bufs=4)
+            nc.gpsimd.tensor_scalar(out=var[:], in0=ss[i][:], scalar1=1.0 / D, scalar2=EPS, op0=ALU.mult, op1=ALU.add)
+            nc.gpsimd.tensor_tensor(out=rstd[i][:], in0=var[:], in1=neg_half[:], op=ALU.pow)
+
+        def norm_pass(i):
+            o = work.tile([P, D], F32, name="o", bufs=4)
+            flat = r[i][:].rearrange("p m t -> p (m t)")
+            if i in NORM_ON_SCALAR:
+                nb = work.tile([P, 1], F32, name="nb", bufs=4)
+                nc.gpsimd.tensor_tensor(out=nb[:], in0=nm[i][:], in1=rstd[i][:], op=ALU.mult)
+                nc.scalar.activation(out=o[:], in_=flat, func=ACT.Identity, scale=rstd[i][:], bias=nb[:])
+            else:
+                nc.vector.tensor_scalar(out=o[:], in0=flat, scalar1=nm[i][:], scalar2=rstd[i][:], op0=ALU.add, op1=ALU.mult)
+            nc.sync.dma_start(out=out_rows[:, i, :], in_=o[:])
+
+        permute_words(0, 1)
+        permute_words(1, 1)
+        dequant(0)
+        permute_words(0, 0)
+        permute_words(1, 0)
+        dequant(1)
+        dequant(2)
+        turn(0)
+        copy_out(0)
+        dequant(3)
+        permute_scales(0)
+        turn(1)
+        quant_in(0)
+        permute_scales(1)
+        first_matmuls(0, 0)
+        copy_out(1)
+        dequant(4)
+        first_matmuls(0, 1)
+        exps(0, 0)
+        turn(2)
+        exps(0, 1)
+        quant_in(1)
+        minus_one(0, 0)
+        first_matmuls(1, 0)
+        minus_one(0, 1)
+        copy_out(2)
+        dequant(5)
+        first_matmuls(1, 1)
+        elu_pass(0, 0)
+        elu_pass(0, 1)
+        exps(1, 0)
+        turn(3)
+        exps(1, 1)
+        quant_in(2)
+        gain_pass(0)
+        minus_one(1, 0)
+        first_matmuls(2, 0)
+        minus_one(1, 1)
+        copy_out(3)
+        dequant(6)
+        first_matmuls(2, 1)
+        elu_pass(1, 0)
+        elu_pass(1, 1)
+        quant_m(0)
+        exps(2, 0)
+        turn(4)
+        exps(2, 1)
+        quant_in(3)
+        gain_pass(1)
+        minus_one(2, 0)
+        first_matmuls(3, 0)
+        minus_one(2, 1)
+        second_matmuls(0, 0)
+        copy_out(4)
+        dequant(7)
+        first_matmuls(3, 1)
+        elu_pass(2, 0)
+        elu_pass(2, 1)
+        quant_m(1)
+        exps(3, 0)
+        turn(5)
+        exps(3, 1)
+        quant_in(4)
+        gain_pass(2)
+        gate_tanh(0)
+        second_matmuls(0, 1)
+        minus_one(3, 0)
+        first_matmuls(4, 0)
+        minus_one(3, 1)
+        second_matmuls(1, 0)
+        copy_out(5)
+        gate_pass(0)
+        skip_matmuls(0)
+        first_matmuls(4, 1)
+        elu_pass(3, 0)
+        elu_pass(3, 1)
+        quant_m(2)
+        residual_pass(0)
+        exps(4, 0)
+        turn(6)
+        exps(4, 1)
+        quant_in(5)
+        gain_pass(3)
+        gate_tanh(1)
+        second_matmuls(1, 1)
+        minus_one(4, 0)
+        first_matmuls(5, 0)
+        minus_one(4, 1)
+        second_matmuls(2, 0)
+        copy_out(6)
+        gate_pass(1)
+        skip_matmuls(1)
+        first_matmuls(5, 1)
+        elu_pass(4, 0)
+        elu_pass(4, 1)
+        quant_m(3)
+        residual_pass(1)
+        exps(5, 0)
+        squares(0)
+        turn(7)
+        exps(5, 1)
+        quant_in(6)
+        gain_pass(4)
+        gate_tanh(2)
+        second_matmuls(2, 1)
+        minus_one(5, 0)
+        first_matmuls(6, 0)
+        minus_one(5, 1)
+        second_matmuls(3, 0)
+        copy_out(7)
+        gate_pass(2)
+        skip_matmuls(2)
+        first_matmuls(6, 1)
+        elu_pass(5, 0)
+        elu_pass(5, 1)
+        scale_up(0)
+        quant_m(4)
+        residual_pass(2)
+        exps(6, 0)
+        squares(1)
+        exps(6, 1)
+        quant_in(7)
+        gain_pass(5)
+        gate_tanh(3)
+        second_matmuls(3, 1)
+        minus_one(6, 0)
+        first_matmuls(7, 0)
+        minus_one(6, 1)
+        second_matmuls(4, 0)
+        gate_pass(3)
+        norm_pass(0)
+        skip_matmuls(3)
+        first_matmuls(7, 1)
+        elu_pass(6, 0)
+        elu_pass(6, 1)
+        scale_up(1)
+        quant_m(5)
+        residual_pass(3)
+        exps(7, 0)
+        squares(2)
+        exps(7, 1)
+        gain_pass(6)
+        gate_tanh(4)
+        second_matmuls(4, 1)
+        minus_one(7, 0)
+        minus_one(7, 1)
+        second_matmuls(5, 0)
+        gate_pass(4)
+        norm_pass(1)
+        skip_matmuls(4)
+        elu_pass(7, 0)
+        elu_pass(7, 1)
+        scale_up(2)
+        quant_m(6)
+        residual_pass(4)
+        squares(3)
+        gain_pass(7)
+        gate_tanh(5)
+        second_matmuls(5, 1)
+        second_matmuls(6, 0)
+        gate_pass(5)
+        norm_pass(2)
+        skip_matmuls(5)
+        scale_up(3)
+        quant_m(7)
+        residual_pass(5)
+        squares(4)
+        gate_tanh(6)
+        second_matmuls(6, 1)
+        second_matmuls(7, 0)
+        gate_pass(6)
+        norm_pass(3)
+        skip_matmuls(6)
+        scale_up(4)
+        residual_pass(6)
+        squares(5)
+        gate_tanh(7)
+        norm_pass(4)
+        second_matmuls(7, 1)
+        skip_matmuls(7)
+        gate_pass(7)
+        scale_up(5)
+        squares(6)
+        residual_pass(7)
+        norm_pass(5)
+        scale_up(6)
+        squares(7)
+        norm_pass(6)
+        scale_up(7)
+        norm_pass(7)

@@ -20,13 +20,16 @@ ACT = mybir.ActivationFunctionType
 
 P = 128
 TILES = N // P
-MINUS_ON_VECTOR = [(0, 0), (1, 1), (2, 1)]
-DEQ_ON_VECTOR = [(4, 0), (4, 1), (4, 2), (4, 3), (5, 0), (5, 1), (5, 2), (5, 3)]
-NORM_ON_SCALAR = [0, 1, 2, 3, 4]
+MINUS_ON_VECTOR = [(1, 0), (1, 1), (2, 1), (3, 1), (4, 0), (6, 1)]
+MINUS_ON_GPSIMD = []
+COPY_ON_VECTOR = [2]
+GAIN_ON_GPSIMD = [1, 2, 3, 4, 5, 6]
+DEQ_ON_VECTOR = [(4, 0), (4, 1), (4, 2), (4, 3), (6, 0), (6, 1), (6, 2), (6, 3), (7, 0), (7, 1), (7, 2), (7, 3)]
+NORM_ON_SCALAR = [1, 2, 4]
 
 
 def ZBANK(i, h):
-    return "z%d" % h if i < 7 else "t0%d" % h
+    return "z%d" % h if i < 6 else "t%d%d" % (i - 6, h)
 
 
 def tile_temporalfusioncontextgatedresidual_d1p_kernel(
@@ -52,6 +55,7 @@ def tile_temporalfusioncontextgatedresidual_d1p_kernel(
         g_scales = keep.tile([P, 2, H], U8, name="g_scales", align_bytes=64)
         gain_sb = keep.tile([P, 2, 4], BF16, name="gain_sb")
         skip_sb = keep.tile([P, 4], BF16, name="skip_sb")
+        skip_f32 = keep.tile([P, 4], F32, name="skip_f32")
         ident = keep.tile([P, P], F32, name="ident")
         diag = keep.tile([P, 4, P], BF16, name="diag")
         zero = keep.tile([P, 1], F32, name="zero")
@@ -82,21 +86,27 @@ def tile_temporalfusioncontextgatedresidual_d1p_kernel(
         nc.vector.memset(neg_half[:], -0.5)
         nc.vector.memset(minus[:], -1.0)
 
+        nc.scalar.activation(out=warm[:], in_=zero[:], func=ACT.Exp)
         nc.sync.dma_start(out=w_raw[:, 0, :].bitcast(I32), in_=wa_words[0].bitcast(I32))
         nc.sync.dma_start(out=w_raw[:, 1, :].bitcast(I32), in_=wc_words[0].bitcast(I32))
         nc.sync.dma_start(out=c_sc[:], in_=c_scale.rearrange("(p i) q -> p (i q)", i=TILES))
         load_c(*chunks[0])
         load_a(*chunks[0])
+
+        def load_weight_scales(engine, w, q):
+            scales = (wa_scales, wc_scales)[w]
+            engine.dma_start(out=s_raw[32 * q : 32 * q + 4, w, :].bitcast(I32), in_=scales[0, 4 * q : 4 * q + 4, :].bitcast(I32))
+
+        for q in range(2):
+            load_weight_scales(nc.gpsimd, 1, q)
         make_identity(nc, ident[:])
-        for w, scales in ((1, wc_scales), (0, wa_scales)):
-            for q in range(4):
-                (nc.sync, nc.scalar)[w].dma_start(
-                    out=s_raw[32 * q : 32 * q + 4, w, :].bitcast(I32), in_=scales[0, 4 * q : 4 * q + 4, :].bitcast(I32)
-                )
-        nc.scalar.activation(out=warm[:], in_=zero[:], func=ACT.Exp)
+        for q in range(2, 4):
+            load_weight_scales(nc.gpsimd, 1, q)
+        for q in range(4):
+            load_weight_scales(nc.sync, 0, q)
+        nc.sync.dma_start(out=skip_sb[:], in_=skip.rearrange("(p t) -> p t", t=4))
         load_c(*chunks[1])
         load_a(*chunks[1])
-        nc.sync.dma_start(out=skip_sb[:], in_=skip.rearrange("(p t) -> p t", t=4))
         nc.sync.dma_start(out=gain_sb[:], in_=gain.rearrange("(g p t) -> p g t", g=2, t=4))
         load_c(*chunks[2])
         load_a(*chunks[2])
@@ -108,10 +118,10 @@ def tile_temporalfusioncontextgatedresidual_d1p_kernel(
         for g in range(2):
             nc.sync.dma_start(out=g_words[:, g, :].bitcast(I32), in_=wgv_words[g].bitcast(I32))
 
-        for t in range(4):
-            nc.gpsimd.tensor_scalar(
-                out=diag[:, t, :], in0=ident[:], scalar1=skip_sb[:, t : t + 1], scalar2=0.0, op0=ALU.mult, op1=ALU.add
-            )
+        def build_diagonals():
+            nc.scalar.copy(out=skip_f32[:], in_=skip_sb[:])
+            for t in range(4):
+                nc.scalar.activation(out=diag[:, t, :], in_=ident[:], func=ACT.Copy, scale=skip_f32[:, t : t + 1])
 
         def permute_words(w, g):
             nc.vector.tensor_copy(
@@ -147,7 +157,7 @@ def tile_temporalfusioncontextgatedresidual_d1p_kernel(
 
         def copy_out(i):
             grp[i] = work.tile([P, 2 * D], BF16, name="grp", bufs=8, align_bytes=64)
-            nc.scalar.copy(
+            (nc.vector.tensor_copy if i in COPY_ON_VECTOR else nc.scalar.copy)(
                 out=grp[i][:].bitcast(F32).rearrange("p (o r u) -> p o r u", o=2, u=2),
                 in_=tr[i][:].rearrange("p (o u) r -> p o r u", o=2),
             )
@@ -173,7 +183,7 @@ def tile_temporalfusioncontextgatedresidual_d1p_kernel(
                         )
 
         def exps(i, g):
-            e[i, g] = work.tile([P, P, 4], F32, name="e%d" % g, bufs=3)
+            e[i, g] = work.tile([P, P, 4], F32, name="e%d" % g, bufs=4)
             nc.scalar.activation(out=e[i, g][:], in_=tb[i, g][:].rearrange("p (t n) -> p n t", t=4), func=ACT.Exp)
 
         def minus_one(i, g):
@@ -186,12 +196,21 @@ def tile_temporalfusioncontextgatedresidual_d1p_kernel(
                     scalar2=None,
                     op0=ALU.subtract,
                 )
+            elif (i, g) in MINUS_ON_GPSIMD:
+                nc.gpsimd.tensor_scalar(
+                    out=n[i, g][:].rearrange("p n t -> p (n t)"),
+                    in0=e[i, g][:].rearrange("p n t -> p (n t)"),
+                    scalar1=-1.0,
+                    scalar2=1.0,
+                    op0=ALU.add,
+                    op1=ALU.mult,
+                )
             else:
                 nc.scalar.activation(out=n[i, g][:], in_=e[i, g][:], func=ACT.Identity, bias=minus[:])
 
         def elu_pass(i, g):
             if i not in elu:
-                elu[i] = work.tile([P, 2, P, 4], F32, name="elu", bufs=3)
+                elu[i] = work.tile([P, 2, P, 4], F32, name="elu", bufs=4)
             nc.vector.scalar_tensor_tensor(
                 out=elu[i][:, g, :, :],
                 in0=tb[i, g][:].rearrange("p (t n) -> p n t", t=4),
@@ -202,8 +221,8 @@ def tile_temporalfusioncontextgatedresidual_d1p_kernel(
             )
 
         def gain_pass(i):
-            mb[i] = work.tile([P, 2, P, 4], BF16, name="mb", bufs=3, align_bytes=64)
-            nc.vector.tensor_tensor(
+            mb[i] = work.tile([P, 2, P, 4], BF16, name="mb", bufs=4, align_bytes=64)
+            (nc.gpsimd if i in GAIN_ON_GPSIMD else nc.vector).tensor_tensor(
                 out=mb[i][:], in0=elu[i][:], in1=gain_sb[:].unsqueeze(2).to_broadcast([P, 2, P, 4]), op=ALU.mult
             )
 
@@ -229,7 +248,7 @@ def tile_temporalfusioncontextgatedresidual_d1p_kernel(
                     )
 
         def skip_matmuls(i):
-            sa[i] = psum.tile([P, D], F32, name="sa" if i < 7 else "tr")
+            sa[i] = psum.tile([P, D], F32, name="tr" if i == 6 else "sa")
             a_t = grp[i][:, 0:D].rearrange("p (r t) -> p t r", t=4)
             for t in range(4):
                 nc.tensor.matmul(sa[i][:, P * t : P * (t + 1)], lhsT=a_t[:, t, :], rhs=diag[:, t, :], start=True, stop=True)
@@ -273,7 +292,7 @@ def tile_temporalfusioncontextgatedresidual_d1p_kernel(
             nc.gpsimd.tensor_tensor(out=rstd[i][:], in0=var[:], in1=neg_half[:], op=ALU.pow)
 
         def norm_pass(i):
-            o = work.tile([P, D], F32, name="o", bufs=4)
+            o = work.tile([P, D], F32, name="o", bufs=6)
             flat = r[i][:].rearrange("p m t -> p (m t)")
             if i in NORM_ON_SCALAR:
                 nb = work.tile([P, 1], F32, name="nb", bufs=4)
@@ -286,190 +305,191 @@ def tile_temporalfusioncontextgatedresidual_d1p_kernel(
         permute_words(0, 1)
         permute_words(1, 1)
         dequant(0)
+        dequant(1)
+        turn(0)
         permute_words(0, 0)
         permute_words(1, 0)
-        dequant(1)
-        dequant(2)
-        turn(0)
         copy_out(0)
+        turn(1)
+        dequant(2)
+        permute_scales(1)
+        copy_out(1)
+        quant_in(0)
         dequant(3)
         permute_scales(0)
-        turn(1)
-        quant_in(0)
-        permute_scales(1)
-        first_matmuls(0, 0)
-        copy_out(1)
-        dequant(4)
-        first_matmuls(0, 1)
-        exps(0, 0)
         turn(2)
-        exps(0, 1)
-        quant_in(1)
-        minus_one(0, 0)
-        first_matmuls(1, 0)
-        minus_one(0, 1)
-        copy_out(2)
+        first_matmuls(0, 1)
         dequant(5)
-        first_matmuls(1, 1)
-        elu_pass(0, 0)
-        elu_pass(0, 1)
-        exps(1, 0)
+        copy_out(2)
+        build_diagonals()
+        quant_in(1)
         turn(3)
-        exps(1, 1)
+        exps(0, 1)
         quant_in(2)
-        gain_pass(0)
-        minus_one(1, 0)
-        first_matmuls(2, 0)
-        minus_one(1, 1)
+        dequant(4)
+        first_matmuls(1, 1)
+        skip_matmuls(0)
         copy_out(3)
-        dequant(6)
-        first_matmuls(2, 1)
-        elu_pass(1, 0)
-        elu_pass(1, 1)
-        quant_m(0)
-        exps(2, 0)
+        dequant(7)
+        minus_one(0, 1)
         turn(4)
-        exps(2, 1)
         quant_in(3)
-        gain_pass(1)
-        minus_one(2, 0)
+        exps(1, 1)
+        dequant(6)
+        first_matmuls(0, 0)
+        elu_pass(0, 1)
+        copy_out(4)
+        first_matmuls(1, 0)
+        minus_one(1, 1)
+        exps(0, 0)
+        quant_in(4)
+        first_matmuls(2, 1)
+        minus_one(0, 0)
+        elu_pass(1, 1)
+        turn(5)
+        exps(1, 0)
+        elu_pass(0, 0)
+        first_matmuls(3, 1)
+        copy_out(5)
+        minus_one(1, 0)
+        elu_pass(1, 0)
+        exps(2, 1)
+        turn(6)
+        gain_pass(0)
+        exps(3, 1)
+        first_matmuls(2, 0)
+        copy_out(6)
         first_matmuls(3, 0)
         minus_one(2, 1)
-        second_matmuls(0, 0)
-        copy_out(4)
-        dequant(7)
-        first_matmuls(3, 1)
-        elu_pass(2, 0)
-        elu_pass(2, 1)
-        quant_m(1)
-        exps(3, 0)
-        turn(5)
-        exps(3, 1)
-        quant_in(4)
-        gain_pass(2)
-        gate_tanh(0)
-        second_matmuls(0, 1)
-        minus_one(3, 0)
-        first_matmuls(4, 0)
+        exps(2, 0)
         minus_one(3, 1)
-        second_matmuls(1, 0)
-        copy_out(5)
-        gate_pass(0)
-        skip_matmuls(0)
-        first_matmuls(4, 1)
-        elu_pass(3, 0)
-        elu_pass(3, 1)
-        quant_m(2)
-        residual_pass(0)
-        exps(4, 0)
-        turn(6)
-        exps(4, 1)
-        quant_in(5)
-        gain_pass(3)
-        gate_tanh(1)
-        second_matmuls(1, 1)
-        minus_one(4, 0)
-        first_matmuls(5, 0)
-        minus_one(4, 1)
-        second_matmuls(2, 0)
-        copy_out(6)
-        gate_pass(1)
-        skip_matmuls(1)
-        first_matmuls(5, 1)
-        elu_pass(4, 0)
-        elu_pass(4, 1)
-        quant_m(3)
-        residual_pass(1)
-        exps(5, 0)
-        squares(0)
         turn(7)
-        exps(5, 1)
-        quant_in(6)
-        gain_pass(4)
-        gate_tanh(2)
-        second_matmuls(2, 1)
-        minus_one(5, 0)
-        first_matmuls(6, 0)
-        minus_one(5, 1)
-        second_matmuls(3, 0)
+        quant_m(0)
+        minus_one(2, 0)
+        quant_in(5)
+        second_matmuls(0, 0)
         copy_out(7)
-        gate_pass(2)
-        skip_matmuls(2)
-        first_matmuls(6, 1)
+        quant_in(6)
+        gain_pass(1)
+        elu_pass(2, 0)
+        second_matmuls(0, 1)
+        exps(3, 0)
+        elu_pass(2, 1)
+        first_matmuls(4, 0)
+        minus_one(3, 0)
+        elu_pass(3, 1)
+        first_matmuls(4, 1)
+        exps(4, 0)
+        elu_pass(3, 0)
+        first_matmuls(5, 1)
+        gate_tanh(0)
+        minus_one(4, 0)
+        exps(4, 1)
+        first_matmuls(5, 0)
+        quant_m(1)
+        gate_pass(0)
+        gain_pass(2)
+        minus_one(4, 1)
+        second_matmuls(1, 0)
+        elu_pass(4, 0)
+        exps(5, 0)
+        second_matmuls(1, 1)
+        residual_pass(0)
+        first_matmuls(6, 0)
+        minus_one(5, 0)
+        elu_pass(4, 1)
+        gate_tanh(1)
+        skip_matmuls(1)
+        gain_pass(3)
+        skip_matmuls(6)
         elu_pass(5, 0)
-        elu_pass(5, 1)
-        scale_up(0)
-        quant_m(4)
-        residual_pass(2)
         exps(6, 0)
-        squares(1)
-        exps(6, 1)
-        quant_in(7)
-        gain_pass(5)
-        gate_tanh(3)
-        second_matmuls(3, 1)
+        first_matmuls(6, 1)
+        gate_pass(1)
         minus_one(6, 0)
+        squares(0)
+        residual_pass(1)
+        elu_pass(6, 0)
+        exps(5, 1)
+        skip_matmuls(2)
+        scale_up(0)
+        quant_m(2)
+        minus_one(5, 1)
+        quant_m(3)
+        second_matmuls(2, 0)
+        squares(1)
+        quant_in(7)
+        second_matmuls(2, 1)
+        gain_pass(4)
+        elu_pass(5, 1)
+        gate_tanh(2)
         first_matmuls(7, 0)
+        exps(6, 1)
+        gate_pass(2)
+        second_matmuls(3, 0)
+        exps(7, 0)
+        residual_pass(2)
+        first_matmuls(7, 1)
+        minus_one(7, 0)
+        second_matmuls(3, 1)
+        scale_up(1)
         minus_one(6, 1)
+        gate_tanh(3)
+        quant_m(4)
+        skip_matmuls(3)
+        elu_pass(7, 0)
+        gain_pass(5)
+        squares(2)
         second_matmuls(4, 0)
         gate_pass(3)
-        norm_pass(0)
-        skip_matmuls(3)
-        first_matmuls(7, 1)
-        elu_pass(6, 0)
-        elu_pass(6, 1)
-        scale_up(1)
-        quant_m(5)
-        residual_pass(3)
-        exps(7, 0)
-        squares(2)
-        exps(7, 1)
-        gain_pass(6)
         gate_tanh(4)
+        elu_pass(6, 1)
         second_matmuls(4, 1)
-        minus_one(7, 0)
-        minus_one(7, 1)
-        second_matmuls(5, 0)
-        gate_pass(4)
         norm_pass(1)
+        residual_pass(3)
+        exps(7, 1)
+        gate_pass(4)
         skip_matmuls(4)
-        elu_pass(7, 0)
-        elu_pass(7, 1)
         scale_up(2)
-        quant_m(6)
-        residual_pass(4)
+        minus_one(7, 1)
+        quant_m(5)
         squares(3)
-        gain_pass(7)
-        gate_tanh(5)
+        norm_pass(0)
+        second_matmuls(5, 0)
+        residual_pass(4)
+        gain_pass(6)
         second_matmuls(5, 1)
-        second_matmuls(6, 0)
+        gate_tanh(5)
+        elu_pass(7, 1)
+        skip_matmuls(5)
+        squares(4)
         gate_pass(5)
         norm_pass(2)
-        skip_matmuls(5)
-        scale_up(3)
-        quant_m(7)
         residual_pass(5)
-        squares(4)
-        gate_tanh(6)
-        second_matmuls(6, 1)
-        second_matmuls(7, 0)
-        gate_pass(6)
-        norm_pass(3)
-        skip_matmuls(6)
-        scale_up(4)
-        residual_pass(6)
+        scale_up(3)
+        quant_m(6)
         squares(5)
-        gate_tanh(7)
-        norm_pass(4)
-        second_matmuls(7, 1)
         skip_matmuls(7)
-        gate_pass(7)
+        gain_pass(7)
+        second_matmuls(6, 0)
+        scale_up(4)
+        second_matmuls(6, 1)
+        gate_tanh(6)
         scale_up(5)
+        quant_m(7)
+        norm_pass(4)
+        gate_pass(6)
+        second_matmuls(7, 0)
+        second_matmuls(7, 1)
+        gate_tanh(7)
+        residual_pass(6)
+        gate_pass(7)
         squares(6)
         residual_pass(7)
-        norm_pass(5)
         scale_up(6)
+        norm_pass(3)
         squares(7)
+        norm_pass(5)
         norm_pass(6)
         scale_up(7)
         norm_pass(7)

@@ -20,12 +20,12 @@ ACT = mybir.ActivationFunctionType
 
 P = 128
 TILES = N // P
-MINUS_ON_VECTOR = [(1, 0), (1, 1), (2, 1), (3, 1), (4, 0), (6, 1)]
+MINUS_ON_VECTOR = [(0, 0), (1, 1)]
 MINUS_ON_GPSIMD = []
-COPY_ON_VECTOR = [2]
-GAIN_ON_GPSIMD = [1, 2, 3, 4, 5, 6]
-DEQ_ON_VECTOR = [(4, 0), (4, 1), (4, 2), (4, 3), (6, 0), (6, 1), (6, 2), (6, 3), (7, 0), (7, 1), (7, 2), (7, 3)]
-NORM_ON_SCALAR = [1, 2, 4]
+COPY_ON_VECTOR = []
+GAIN_ON_GPSIMD = []
+DEQ_ON_VECTOR = [(3, 0), (3, 1), (3, 2), (3, 3), (4, 0), (4, 1), (4, 2), (4, 3)]
+NORM_ON_SCALAR = [0, 1, 3, 5]
 
 
 def ZBANK(i, h):
@@ -63,22 +63,22 @@ def tile_temporalfusioncontextgatedresidual_d1p_kernel(
         warm = keep.tile([P, 1], F32, name="warm")
         neg_half = keep.tile([P, 1], F32, name="neg_half")
 
-        chunks = [(0, 2), (2, 4), (4, 8)]
-        a_sb, cb_sb = {}, {}
-        for lo, hi in chunks:
-            a_chunk = keep.tile([P, hi - lo, D], BF16, name="a_chunk%d" % lo)
-            cb_chunk = keep.tile([P, hi - lo, D], U8, name="cb_chunk%d" % lo)
+        a_chunks, c_chunks = ((0, 2), (2, 4), (4, 8)), ((0, 4), (4, 8))
+        a_in, c_in, a_sb, cb_sb = {}, {}, {}, {}
+        for lo, hi in a_chunks:
+            a_in[lo] = keep.tile([P, hi - lo, D], BF16, name="a_in%d" % lo)
             for i in range(lo, hi):
-                a_sb[i] = a_chunk[:, i - lo, :]
-                cb_sb[i] = cb_chunk[:, i - lo, :]
-            a_sb["c%d" % lo] = a_chunk
-            cb_sb["c%d" % lo] = cb_chunk
+                a_sb[i] = a_in[lo][:, i - lo, :]
+        for lo, hi in c_chunks:
+            c_in[lo] = keep.tile([P, hi - lo, D], U8, name="c_in%d" % lo)
+            for i in range(lo, hi):
+                cb_sb[i] = c_in[lo][:, i - lo, :]
 
         def load_a(lo, hi):
-            nc.sync.dma_start(out=a_sb["c%d" % lo][:], in_=a_rows[:, lo:hi, :])
+            nc.sync.dma_start(out=a_in[lo][:], in_=a_rows[:, lo:hi, :])
 
         def load_c(lo, hi):
-            nc.sync.dma_start(out=cb_sb["c%d" % lo][:], in_=c_rows[:, lo:hi, :])
+            nc.sync.dma_start(out=c_in[lo][:], in_=c_rows[:, lo:hi, :])
 
         nc.vector.memset(zero[:], 0.0)
         nc.vector.memset(s_raw[:].rearrange("p w n -> p (w n)").bitcast(I32), 0)
@@ -86,30 +86,27 @@ def tile_temporalfusioncontextgatedresidual_d1p_kernel(
         nc.vector.memset(neg_half[:], -0.5)
         nc.vector.memset(minus[:], -1.0)
 
-        nc.scalar.activation(out=warm[:], in_=zero[:], func=ACT.Exp)
-        nc.sync.dma_start(out=w_raw[:, 0, :].bitcast(I32), in_=wa_words[0].bitcast(I32))
-        nc.sync.dma_start(out=w_raw[:, 1, :].bitcast(I32), in_=wc_words[0].bitcast(I32))
-        nc.sync.dma_start(out=c_sc[:], in_=c_scale.rearrange("(p i) q -> p (i q)", i=TILES))
-        load_c(*chunks[0])
-        load_a(*chunks[0])
-
         def load_weight_scales(engine, w, q):
             scales = (wa_scales, wc_scales)[w]
             engine.dma_start(out=s_raw[32 * q : 32 * q + 4, w, :].bitcast(I32), in_=scales[0, 4 * q : 4 * q + 4, :].bitcast(I32))
 
-        for q in range(2):
-            load_weight_scales(nc.gpsimd, 1, q)
         make_identity(nc, ident[:])
-        for q in range(2, 4):
-            load_weight_scales(nc.gpsimd, 1, q)
+        nc.sync.dma_start(out=c_sc[:], in_=c_scale.rearrange("(p i) q -> p (i q)", i=TILES))
+        load_c(*c_chunks[0])
+        for q in range(3):
+            load_weight_scales(nc.scalar, 1, q)
+        nc.scalar.activation(out=warm[:], in_=zero[:], func=ACT.Exp)
+        load_a(*a_chunks[0])
+        for w, words in enumerate((wa_words, wc_words)):
+            nc.sync.dma_start(out=w_raw[:, w, :].bitcast(I32), in_=words[0].bitcast(I32))
+        load_weight_scales(nc.sync, 1, 3)
         for q in range(4):
             load_weight_scales(nc.sync, 0, q)
+        load_a(*a_chunks[1])
         nc.sync.dma_start(out=skip_sb[:], in_=skip.rearrange("(p t) -> p t", t=4))
-        load_c(*chunks[1])
-        load_a(*chunks[1])
         nc.sync.dma_start(out=gain_sb[:], in_=gain.rearrange("(g p t) -> p g t", g=2, t=4))
-        load_c(*chunks[2])
-        load_a(*chunks[2])
+        load_c(*c_chunks[1])
+        load_a(*a_chunks[2])
         for q in range(4):
             nc.sync.dma_start(
                 out=g_scales[32 * q : 32 * q + 4, :, :].bitcast(I32),
@@ -149,7 +146,7 @@ def tile_temporalfusioncontextgatedresidual_d1p_kernel(
                     nc.scalar.activation(out=cw[i][:, blk], in_=cb_sb[i][:, blk].bitcast(F8), func=ACT.Copy, scale=scale)
 
         def turn(i):
-            tr[i] = psum.tile([P, 4, P], F32, name="tr")
+            tr[i] = psum.tile([P, 4, P], F32, name={1: "sa", 2: "z0", 3: "z1"}.get(i, "tr"))
             for s, rows in enumerate((a_sb[i], cw[i][:])):
                 words = rows.bitcast(F32)
                 for u in range(2):
@@ -277,219 +274,220 @@ def tile_temporalfusioncontextgatedresidual_d1p_kernel(
             )
 
         def squares(i):
-            nm[i] = work.tile([P, 1], F32, name="nm", bufs=8)
             ss[i] = work.tile([P, 1], F32, name="ss", bufs=8)
+            nm[i] = work.tile([P, 1], F32, name="nm", bufs=8)
             sq = work.tile([P, D], F32, name="sq", bufs=2)
-            nc.scalar.mul(nm[i][:], rsum[i][:], -1.0 / D)
-            nc.scalar.activation(
-                out=sq[:], in_=r[i][:].rearrange("p m t -> p (m t)"), func=ACT.Square, bias=nm[i][:], accum_out=ss[i][:]
-            )
+            flat = r[i][:].rearrange("p m t -> p (m t)")
+            nc.scalar.activation(out=sq[:], in_=flat, func=ACT.Square, scale=-float(D), bias=rsum[i][:], accum_out=ss[i][:])
+            nc.gpsimd.tensor_scalar(out=nm[i][:], in0=rsum[i][:], scalar1=-1.0 / D, scalar2=1.0, op0=ALU.mult, op1=ALU.mult)
 
         def scale_up(i):
             rstd[i] = work.tile([P, 1], F32, name="rstd", bufs=8)
             var = work.tile([P, 1], F32, name="var", bufs=4)
-            nc.gpsimd.tensor_scalar(out=var[:], in0=ss[i][:], scalar1=1.0 / D, scalar2=EPS, op0=ALU.mult, op1=ALU.add)
+            engine = nc.vector if i == TILES - 1 else nc.gpsimd
+            engine.tensor_scalar(out=var[:], in0=ss[i][:], scalar1=1.0 / D**3, scalar2=EPS, op0=ALU.mult, op1=ALU.add)
             nc.gpsimd.tensor_tensor(out=rstd[i][:], in0=var[:], in1=neg_half[:], op=ALU.pow)
+            if i in NORM_ON_SCALAR:
+                nb[i] = work.tile([P, 1], F32, name="nb", bufs=8)
+                nc.gpsimd.tensor_tensor(out=nb[i][:], in0=nm[i][:], in1=rstd[i][:], op=ALU.mult)
 
         def norm_pass(i):
             o = work.tile([P, D], F32, name="o", bufs=6)
             flat = r[i][:].rearrange("p m t -> p (m t)")
             if i in NORM_ON_SCALAR:
-                nb = work.tile([P, 1], F32, name="nb", bufs=4)
-                nc.gpsimd.tensor_tensor(out=nb[:], in0=nm[i][:], in1=rstd[i][:], op=ALU.mult)
-                nc.scalar.activation(out=o[:], in_=flat, func=ACT.Identity, scale=rstd[i][:], bias=nb[:])
+                nc.scalar.activation(out=o[:], in_=flat, func=ACT.Identity, scale=rstd[i][:], bias=nb[i][:])
             else:
                 nc.vector.tensor_scalar(out=o[:], in0=flat, scalar1=nm[i][:], scalar2=rstd[i][:], op0=ALU.add, op1=ALU.mult)
             nc.sync.dma_start(out=out_rows[:, i, :], in_=o[:])
 
-        permute_words(0, 1)
-        permute_words(1, 1)
         dequant(0)
+        dequant(3)
         dequant(1)
         turn(0)
+        permute_words(0, 1)
+        permute_words(1, 1)
+        dequant(2)
+        turn(1)
         permute_words(0, 0)
         permute_words(1, 0)
         copy_out(0)
-        turn(1)
-        dequant(2)
-        permute_scales(1)
         copy_out(1)
-        quant_in(0)
-        dequant(3)
-        permute_scales(0)
-        turn(2)
-        first_matmuls(0, 1)
-        dequant(5)
-        copy_out(2)
         build_diagonals()
-        quant_in(1)
+        turn(2)
+        permute_scales(0)
         turn(3)
-        exps(0, 1)
+        copy_out(2)
+        quant_in(0)
+        permute_scales(1)
+        dequant(5)
+        first_matmuls(0, 0)
+        quant_in(1)
+        first_matmuls(0, 1)
+        exps(0, 0)
         quant_in(2)
         dequant(4)
+        first_matmuls(1, 0)
+        exps(0, 1)
+        minus_one(0, 0)
         first_matmuls(1, 1)
         skip_matmuls(0)
-        copy_out(3)
-        dequant(7)
         minus_one(0, 1)
-        turn(4)
-        quant_in(3)
-        exps(1, 1)
-        dequant(6)
-        first_matmuls(0, 0)
-        elu_pass(0, 1)
-        copy_out(4)
-        first_matmuls(1, 0)
-        minus_one(1, 1)
-        exps(0, 0)
-        quant_in(4)
-        first_matmuls(2, 1)
-        minus_one(0, 0)
-        elu_pass(1, 1)
-        turn(5)
-        exps(1, 0)
         elu_pass(0, 0)
-        first_matmuls(3, 1)
-        copy_out(5)
-        minus_one(1, 0)
-        elu_pass(1, 0)
-        exps(2, 1)
-        turn(6)
-        gain_pass(0)
-        exps(3, 1)
+        turn(4)
+        copy_out(3)
+        elu_pass(0, 1)
         first_matmuls(2, 0)
-        copy_out(6)
-        first_matmuls(3, 0)
-        minus_one(2, 1)
+        exps(1, 0)
+        quant_in(3)
+        gain_pass(0)
+        exps(1, 1)
+        first_matmuls(2, 1)
+        minus_one(1, 0)
+        minus_one(1, 1)
+        copy_out(4)
+        elu_pass(1, 0)
         exps(2, 0)
-        minus_one(3, 1)
-        turn(7)
+        turn(5)
+        elu_pass(1, 1)
+        exps(2, 1)
         quant_m(0)
-        minus_one(2, 0)
-        quant_in(5)
-        second_matmuls(0, 0)
-        copy_out(7)
-        quant_in(6)
+        first_matmuls(3, 0)
         gain_pass(1)
+        minus_one(2, 0)
+        first_matmuls(3, 1)
+        minus_one(2, 1)
+        second_matmuls(0, 0)
+        quant_in(4)
+        copy_out(5)
         elu_pass(2, 0)
         second_matmuls(0, 1)
         exps(3, 0)
         elu_pass(2, 1)
         first_matmuls(4, 0)
-        minus_one(3, 0)
-        elu_pass(3, 1)
-        first_matmuls(4, 1)
-        exps(4, 0)
-        elu_pass(3, 0)
-        first_matmuls(5, 1)
-        gate_tanh(0)
-        minus_one(4, 0)
-        exps(4, 1)
-        first_matmuls(5, 0)
+        dequant(6)
         quant_m(1)
-        gate_pass(0)
+        first_matmuls(4, 1)
         gain_pass(2)
-        minus_one(4, 1)
+        gate_tanh(0)
+        turn(6)
+        exps(3, 1)
+        gate_pass(0)
         second_matmuls(1, 0)
-        elu_pass(4, 0)
-        exps(5, 0)
+        minus_one(3, 0)
+        quant_in(5)
         second_matmuls(1, 1)
         residual_pass(0)
-        first_matmuls(6, 0)
-        minus_one(5, 0)
-        elu_pass(4, 1)
-        gate_tanh(1)
+        minus_one(3, 1)
+        elu_pass(3, 0)
+        exps(4, 0)
         skip_matmuls(1)
-        gain_pass(3)
-        skip_matmuls(6)
-        elu_pass(5, 0)
-        exps(6, 0)
-        first_matmuls(6, 1)
-        gate_pass(1)
-        minus_one(6, 0)
-        squares(0)
-        residual_pass(1)
-        elu_pass(6, 0)
-        exps(5, 1)
-        skip_matmuls(2)
-        scale_up(0)
+        elu_pass(3, 1)
+        gate_tanh(1)
+        first_matmuls(5, 0)
         quant_m(2)
-        minus_one(5, 1)
-        quant_m(3)
+        exps(4, 1)
+        first_matmuls(5, 1)
+        gain_pass(3)
+        exps(5, 0)
         second_matmuls(2, 0)
-        squares(1)
-        quant_in(7)
+        minus_one(4, 0)
+        gate_pass(1)
+        copy_out(6)
+        elu_pass(4, 0)
         second_matmuls(2, 1)
-        gain_pass(4)
-        elu_pass(5, 1)
+        minus_one(4, 1)
+        quant_in(6)
+        residual_pass(1)
+        dequant(7)
+        first_matmuls(6, 0)
+        elu_pass(4, 1)
+        skip_matmuls(2)
         gate_tanh(2)
-        first_matmuls(7, 0)
-        exps(6, 1)
-        gate_pass(2)
+        turn(7)
+        quant_m(3)
+        exps(5, 1)
+        gain_pass(4)
+        minus_one(5, 0)
+        first_matmuls(6, 1)
+        copy_out(7)
         second_matmuls(3, 0)
-        exps(7, 0)
+        gate_pass(2)
+        minus_one(5, 1)
+        skip_matmuls(6)
+        quant_in(7)
+        elu_pass(5, 0)
+        second_matmuls(3, 1)
+        squares(0)
+        elu_pass(5, 1)
+        first_matmuls(7, 0)
+        exps(6, 0)
+        scale_up(0)
         residual_pass(2)
         first_matmuls(7, 1)
-        minus_one(7, 0)
-        second_matmuls(3, 1)
-        scale_up(1)
-        minus_one(6, 1)
         gate_tanh(3)
         quant_m(4)
         skip_matmuls(3)
-        elu_pass(7, 0)
+        exps(6, 1)
         gain_pass(5)
-        squares(2)
         second_matmuls(4, 0)
+        minus_one(6, 0)
+        minus_one(6, 1)
         gate_pass(3)
-        gate_tanh(4)
-        elu_pass(6, 1)
+        squares(1)
+        elu_pass(6, 0)
         second_matmuls(4, 1)
-        norm_pass(1)
-        residual_pass(3)
         exps(7, 1)
-        gate_pass(4)
-        skip_matmuls(4)
-        scale_up(2)
-        minus_one(7, 1)
+        scale_up(1)
+        elu_pass(6, 1)
+        exps(7, 0)
+        residual_pass(3)
+        gate_tanh(4)
         quant_m(5)
-        squares(3)
-        norm_pass(0)
-        second_matmuls(5, 0)
-        residual_pass(4)
+        skip_matmuls(4)
         gain_pass(6)
+        minus_one(7, 1)
+        second_matmuls(5, 0)
+        squares(2)
+        gate_pass(4)
+        minus_one(7, 0)
+        scale_up(2)
+        elu_pass(7, 1)
         second_matmuls(5, 1)
         gate_tanh(5)
-        elu_pass(7, 1)
-        skip_matmuls(5)
-        squares(4)
-        gate_pass(5)
-        norm_pass(2)
-        residual_pass(5)
+        elu_pass(7, 0)
+        squares(3)
+        residual_pass(4)
+        norm_pass(0)
         scale_up(3)
         quant_m(6)
-        squares(5)
-        skip_matmuls(7)
+        skip_matmuls(5)
+        squares(4)
         gain_pass(7)
         second_matmuls(6, 0)
+        norm_pass(1)
         scale_up(4)
         second_matmuls(6, 1)
-        gate_tanh(6)
-        scale_up(5)
+        gate_pass(5)
+        norm_pass(3)
         quant_m(7)
-        norm_pass(4)
-        gate_pass(6)
+        gate_tanh(6)
+        residual_pass(5)
         second_matmuls(7, 0)
         second_matmuls(7, 1)
+        gate_pass(6)
+        squares(5)
+        skip_matmuls(7)
         gate_tanh(7)
         residual_pass(6)
+        scale_up(5)
         gate_pass(7)
         squares(6)
+        norm_pass(5)
         residual_pass(7)
         scale_up(6)
-        norm_pass(3)
+        norm_pass(2)
         squares(7)
-        norm_pass(5)
+        norm_pass(4)
         norm_pass(6)
         scale_up(7)
         norm_pass(7)

from contextlib import ExitStack

import concourse.mybir as mybir
from concourse.masks import make_identity

N, D, H = 1024, 512, 1024
EPS = 1e-5
FLOPS = 2 * N * D * H * 2 + 2 * N * H * 2 * D

F32 = mybir.dt.float32
BF16 = mybir.dt.bfloat16
I32 = mybir.dt.int32
U32 = mybir.dt.uint32
U8 = mybir.dt.uint8
F8 = mybir.dt.float8_e4m3fn
FP8X4 = mybir.dt.float8_e4m3fn_x4
FP4X4 = mybir.dt.float4_e2m1fn_x4
ALU = mybir.AluOpType
ACT = mybir.ActivationFunctionType

P = 128
TILES = N // P
MINUS_ON_VECTOR = [(0, 0), (1, 1)]
MINUS_ON_GPSIMD = []
COPY_ON_VECTOR = []
GAIN_ON_GPSIMD = []
DEQ_ON_VECTOR = [(3, 0), (3, 1), (3, 2), (3, 3), (4, 0), (4, 1), (4, 2), (4, 3)]
NORM_ON_SCALAR = [0, 1, 3, 5]


def ZBANK(i, h):
    return "z%d" % h if i < 6 else "t%d%d" % (i - 6, h)


def tile_temporalfusioncontextgatedresidual_d1p_kernel(
    tc, a, c_bytes, c_scale, wa_words, wa_scales, wc_words, wc_scales, gain, wgv_words, wgv_scales, skip, out
):
    nc = tc.nc
    with ExitStack() as ctx:
        keep = ctx.enter_context(tc.tile_pool(name="keep", bufs=1))
        work = ctx.enter_context(tc.tile_pool(name="work", bufs=2))
        psum = ctx.enter_context(tc.psum_pool(name="psum", bufs=1))
        ctx.enter_context(tc.manual_schedule())

        a_rows = a.rearrange("(p i) k -> p i k", i=TILES)
        c_rows = c_bytes.rearrange("(p i) k -> p i k", i=TILES)
        out_rows = out.rearrange("(p i) d -> p i d", i=TILES)

        c_sc = keep.tile([P, TILES * 4], F32, name="c_sc")
        w_raw = keep.tile([P, 2, 2 * H], U8, name="w_raw", align_bytes=64)
        w_perm = keep.tile([P, 2, 8, 2 * P], U8, name="w_perm", align_bytes=64)
        s_raw = keep.tile([P, 2, H], U8, name="s_raw", align_bytes=64)
        s_perm = keep.tile([P, 2, 8, P], U8, name="s_perm", align_bytes=64)
        g_words = keep.tile([P, 2, 2 * H], U8, name="g_words", align_bytes=64)
        g_scales = keep.tile([P, 2, H], U8, name="g_scales", align_bytes=64)
        gain_sb = keep.tile([P, 2, 4], BF16, name="gain_sb")
        skip_sb = keep.tile([P, 4], BF16, name="skip_sb")
        skip_f32 = keep.tile([P, 4], F32, name="skip_f32")
        ident = keep.tile([P, P], F32, name="ident")
        diag = keep.tile([P, 4, P], BF16, name="diag")
        zero = keep.tile([P, 1], F32, name="zero")
        minus = keep.tile([P, 1], F32, name="minus")
        warm = keep.tile([P, 1], F32, name="warm")
        neg_half = keep.tile([P, 1], F32, name="neg_half")

        a_chunks, c_chunks = ((0, 2), (2, 4), (4, 8)), ((0, 4), (4, 8))
        a_in, c_in, a_sb, cb_sb = {}, {}, {}, {}
        for lo, hi in a_chunks:
            a_in[lo] = keep.tile([P, hi - lo, D], BF16, name="a_in%d" % lo)
            for i in range(lo, hi):
                a_sb[i] = a_in[lo][:, i - lo, :]
        for lo, hi in c_chunks:
            c_in[lo] = keep.tile([P, hi - lo, D], U8, name="c_in%d" % lo)
            for i in range(lo, hi):
                cb_sb[i] = c_in[lo][:, i - lo, :]

        def load_a(lo, hi):
            nc.sync.dma_start(out=a_in[lo][:], in_=a_rows[:, lo:hi, :])

        def load_c(lo, hi):
            nc.sync.dma_start(out=c_in[lo][:], in_=c_rows[:, lo:hi, :])

        nc.vector.memset(zero[:], 0.0)
        nc.vector.memset(s_raw[:].rearrange("p w n -> p (w n)").bitcast(I32), 0)
        nc.vector.memset(g_scales[:].rearrange("p w n -> p (w n)").bitcast(I32), 0)
        nc.vector.memset(neg_half[:], -0.5)
        nc.vector.memset(minus[:], -1.0)

        def load_weight_scales(engine, w, q):
            scales = (wa_scales, wc_scales)[w]
            engine.dma_start(out=s_raw[32 * q : 32 * q + 4, w, :].bitcast(I32), in_=scales[0, 4 * q : 4 * q + 4, :].bitcast(I32))

        make_identity(nc, ident[:])
        nc.sync.dma_start(out=c_sc[:], in_=c_scale.rearrange("(p i) q -> p (i q)", i=TILES))
        load_c(*c_chunks[0])
        for q in range(3):
            load_weight_scales(nc.scalar, 1, q)
        nc.scalar.activation(out=warm[:], in_=zero[:], func=ACT.Exp)
        load_a(*a_chunks[0])
        for w, words in enumerate((wa_words, wc_words)):
            nc.sync.dma_start(out=w_raw[:, w, :].bitcast(I32), in_=words[0].bitcast(I32))
        load_weight_scales(nc.sync, 1, 3)
        for q in range(4):
            load_weight_scales(nc.sync, 0, q)
        load_a(*a_chunks[1])
        nc.sync.dma_start(out=skip_sb[:], in_=skip.rearrange("(p t) -> p t", t=4))
        nc.sync.dma_start(out=gain_sb[:], in_=gain.rearrange("(g p t) -> p g t", g=2, t=4))
        load_c(*c_chunks[1])
        load_a(*a_chunks[2])
        for q in range(4):
            nc.sync.dma_start(
                out=g_scales[32 * q : 32 * q + 4, :, :].bitcast(I32),
                in_=wgv_scales[:, 4 * q : 4 * q + 4, :].rearrange("g q n -> q g n").bitcast(I32),
            )
        for g in range(2):
            nc.sync.dma_start(out=g_words[:, g, :].bitcast(I32), in_=wgv_words[g].bitcast(I32))

        def build_diagonals():
            nc.scalar.copy(out=skip_f32[:], in_=skip_sb[:])
            for t in range(4):
                nc.scalar.activation(out=diag[:, t, :], in_=ident[:], func=ACT.Copy, scale=skip_f32[:, t : t + 1])

        def permute_words(w, g):
            nc.vector.tensor_copy(
                out=w_perm[:, w, 4 * g : 4 * g + 4, :].rearrange("p t (m b) -> p t m b", b=2),
                in_=w_raw[:, w, H * g : H * (g + 1)].rearrange("p (m t b) -> p t m b", t=4, b=2),
            )

        def permute_scales(g):
            nc.vector.tensor_copy(
                out=s_perm[:, :, 4 * g : 4 * g + 4, :],
                in_=s_raw[:, :, D * g : D * (g + 1)].rearrange("p w (m t) -> p w t m", t=4),
            )

        cw, tr, grp, xc, xs, tb, e, n, elu, mb, mc, ms = ({} for x in range(12))
        zb, sa, th, u2, r, rsum, nm, ss, rstd, nb = ({} for x in range(10))

        def dequant(i):
            cw[i] = work.tile([P, D], BF16, name="cw", bufs=8)
            for b in range(4):
                blk = slice(P * b, P * (b + 1))
                scale = c_sc[:, 4 * i + b : 4 * i + b + 1]
                if (i, b) in DEQ_ON_VECTOR:
                    nc.vector.tensor_scalar(out=cw[i][:, blk], in0=cb_sb[i][:, blk].bitcast(F8), scalar1=scale, scalar2=None, op0=ALU.mult)
                else:
                    nc.scalar.activation(out=cw[i][:, blk], in_=cb_sb[i][:, blk].bitcast(F8), func=ACT.Copy, scale=scale)

        def turn(i):
            tr[i] = psum.tile([P, 4, P], F32, name={1: "sa", 2: "z0", 3: "z1"}.get(i, "tr"))
            for s, rows in enumerate((a_sb[i], cw[i][:])):
                words = rows.bitcast(F32)
                for u in range(2):
                    nc.tensor.transpose(tr[i][:, 2 * s + u, :], words[:, u::2], ident[:])

        def copy_out(i):
            grp[i] = work.tile([P, 2 * D], BF16, name="grp", bufs=8, align_bytes=64)
            (nc.vector.tensor_copy if i in COPY_ON_VECTOR else nc.scalar.copy)(
                out=grp[i][:].bitcast(F32).rearrange("p (o r u) -> p o r u", o=2, u=2),
                in_=tr[i][:].rearrange("p (o u) r -> p o r u", o=2),
            )

        def quant_in(i):
            xc[i] = work.tile([P, 2 * P], U32, name="xc", bufs=8, align_bytes=64)
            xs[i] = work.tile([P, 2 * P], U8, name="xs", bufs=8, align_bytes=64)
            nc.vector.quantize_mx(out=xc[i][:].bitcast(FP8X4), scales=xs[i][:], in_=grp[i][:])

        def first_matmuls(i, g):
            if True:
                tb[i, g] = psum.tile([P, 4 * P], F32, name="t%d%d" % (i % 2, g))
                for t in range(4):
                    for w in range(2):
                        nc.tensor.matmul_mx(
                            out=tb[i, g][:, P * t : P * (t + 1)],
                            lhsT=w_perm[:, w, 4 * g + t, :].bitcast(FP4X4),
                            lhsT_scale=s_perm[:, w, 4 * g + t, :],
                            rhs=xc[i][:, P * w : P * (w + 1)].bitcast(FP8X4),
                            rhs_scale=xs[i][:, P * w : P * (w + 1)],
                            start=(w == 0),
                            stop=(w == 1),
                        )

        def exps(i, g):
            e[i, g] = work.tile([P, P, 4], F32, name="e%d" % g, bufs=4)
            nc.scalar.activation(out=e[i, g][:], in_=tb[i, g][:].rearrange("p (t n) -> p n t", t=4), func=ACT.Exp)

        def minus_one(i, g):
            n[i, g] = work.tile([P, P, 4], F32, name="n%d" % g, bufs=4)
            if (i, g) in MINUS_ON_VECTOR:
                nc.vector.tensor_scalar(
                    out=n[i, g][:].rearrange("p n t -> p (n t)"),
                    in0=e[i, g][:].rearrange("p n t -> p (n t)"),
                    scalar1=1.0,
                    scalar2=None,
                    op0=ALU.subtract,
                )
            elif (i, g) in MINUS_ON_GPSIMD:
                nc.gpsimd.tensor_scalar(
                    out=n[i, g][:].rearrange("p n t -> p (n t)"),
                    in0=e[i, g][:].rearrange("p n t -> p (n t)"),
                    scalar1=-1.0,
                    scalar2=1.0,
                    op0=ALU.add,
                    op1=ALU.mult,
                )
            else:
                nc.scalar.activation(out=n[i, g][:], in_=e[i, g][:], func=ACT.Identity, bias=minus[:])

        def elu_pass(i, g):
            if i not in elu:
                elu[i] = work.tile([P, 2, P, 4], F32, name="elu", bufs=4)
            nc.vector.scalar_tensor_tensor(
                out=elu[i][:, g, :, :],
                in0=tb[i, g][:].rearrange("p (t n) -> p n t", t=4),
                scalar=0.0,
                in1=n[i, g][:],
                op0=ALU.max,
                op1=ALU.min,
            )

        def gain_pass(i):
            mb[i] = work.tile([P, 2, P, 4], BF16, name="mb", bufs=4, align_bytes=64)
            (nc.gpsimd if i in GAIN_ON_GPSIMD else nc.vector).tensor_tensor(
                out=mb[i][:], in0=elu[i][:], in1=gain_sb[:].unsqueeze(2).to_broadcast([P, 2, P, 4]), op=ALU.mult
            )

        def quant_m(i):
            mc[i] = work.tile([P, 2 * P], U32, name="mc", bufs=3, align_bytes=64)
            ms[i] = work.tile([P, 2 * P], U8, name="ms", bufs=3, align_bytes=64)
            nc.vector.quantize_mx(
                out=mc[i][:].bitcast(FP8X4), scales=ms[i][:], in_=mb[i][:].rearrange("p g n t -> p (g n t)")
            )

        def second_matmuls(i, h):
            if True:
                zb[i, h] = psum.tile([P, D], F32, name=ZBANK(i, h))
                for g in range(2):
                    nc.tensor.matmul_mx(
                        out=zb[i, h][:],
                        lhsT=mc[i][:, P * g : P * (g + 1)].bitcast(FP8X4),
                        lhsT_scale=ms[i][:, P * g : P * (g + 1)],
                        rhs=g_words[:, g, 2 * D * h : 2 * D * (h + 1)].bitcast(FP4X4),
                        rhs_scale=g_scales[:, g, D * h : D * (h + 1)],
                        start=(g == 0),
                        stop=(g == 1),
                    )

        def skip_matmuls(i):
            sa[i] = psum.tile([P, D], F32, name="tr" if i == 6 else "sa")
            a_t = grp[i][:, 0:D].rearrange("p (r t) -> p t r", t=4)
            for t in range(4):
                nc.tensor.matmul(sa[i][:, P * t : P * (t + 1)], lhsT=a_t[:, t, :], rhs=diag[:, t, :], start=True, stop=True)

        def gate_tanh(i):
            th[i] = work.tile([P, D], F32, name="th", bufs=3)
            nc.scalar.activation(out=th[i][:], in_=zb[i, 0][:], func=ACT.Tanh, scale=0.5)

        def gate_pass(i):
            u2[i] = work.tile([P, P, 4], F32, name="u2", bufs=3)
            nc.vector.scalar_tensor_tensor(
                out=u2[i][:].rearrange("p m t -> p (m t)"), in0=th[i][:], scalar=1.0, in1=zb[i, 1][:], op0=ALU.add, op1=ALU.mult
            )

        def residual_pass(i):
            r[i] = work.tile([P, P, 4], F32, name="r", bufs=8)
            rsum[i] = work.tile([P, 1], F32, name="rsum", bufs=8)
            nc.vector.scalar_tensor_tensor(
                out=r[i][:],
                in0=u2[i][:],
                scalar=0.5,
                in1=sa[i][:].rearrange("p (t m) -> p m t", t=4),
                op0=ALU.mult,
                op1=ALU.add,
                accum_out=rsum[i][:],
            )

        def squares(i):
            ss[i] = work.tile([P, 1], F32, name="ss", bufs=8)
            nm[i] = work.tile([P, 1], F32, name="nm", bufs=8)
            sq = work.tile([P, D], F32, name="sq", bufs=2)
            flat = r[i][:].rearrange("p m t -> p (m t)")
            nc.scalar.activation(out=sq[:], in_=flat, func=ACT.Square, scale=-float(D), bias=rsum[i][:], accum_out=ss[i][:])
            nc.gpsimd.tensor_scalar(out=nm[i][:], in0=rsum[i][:], scalar1=-1.0 / D, scalar2=1.0, op0=ALU.mult, op1=ALU.mult)

        def scale_up(i):
            rstd[i] = work.tile([P, 1], F32, name="rstd", bufs=8)
            var = work.tile([P, 1], F32, name="var", bufs=4)
            engine = nc.vector if i == TILES - 1 else nc.gpsimd
            engine.tensor_scalar(out=var[:], in0=ss[i][:], scalar1=1.0 / D**3, scalar2=EPS, op0=ALU.mult, op1=ALU.add)
            nc.gpsimd.tensor_tensor(out=rstd[i][:], in0=var[:], in1=neg_half[:], op=ALU.pow)
            if i in NORM_ON_SCALAR:
                nb[i] = work.tile([P, 1], F32, name="nb", bufs=8)
                nc.gpsimd.tensor_tensor(out=nb[i][:], in0=nm[i][:], in1=rstd[i][:], op=ALU.mult)

        def norm_pass(i):
            o = work.tile([P, D], F32, name="o", bufs=6)
            flat = r[i][:].rearrange("p m t -> p (m t)")
            if i in NORM_ON_SCALAR:
                nc.scalar.activation(out=o[:], in_=flat, func=ACT.Identity, scale=rstd[i][:], bias=nb[i][:])
            else:
                nc.vector.tensor_scalar(out=o[:], in0=flat, scalar1=nm[i][:], scalar2=rstd[i][:], op0=ALU.add, op1=ALU.mult)
            nc.sync.dma_start(out=out_rows[:, i, :], in_=o[:])

        dequant(0)
        dequant(3)
        dequant(1)
        turn(0)
        permute_words(0, 1)
        permute_words(1, 1)
        dequant(2)
        turn(1)
        permute_words(0, 0)
        permute_words(1, 0)
        copy_out(0)
        copy_out(1)
        build_diagonals()
        turn(2)
        permute_scales(0)
        turn(3)
        copy_out(2)
        quant_in(0)
        permute_scales(1)
        dequant(5)
        first_matmuls(0, 0)
        quant_in(1)
        first_matmuls(0, 1)
        exps(0, 0)
        quant_in(2)
        dequant(4)
        first_matmuls(1, 0)
        exps(0, 1)
        minus_one(0, 0)
        first_matmuls(1, 1)
        skip_matmuls(0)
        minus_one(0, 1)
        elu_pass(0, 0)
        turn(4)
        copy_out(3)
        elu_pass(0, 1)
        first_matmuls(2, 0)
        exps(1, 0)
        quant_in(3)
        gain_pass(0)
        exps(1, 1)
        first_matmuls(2, 1)
        minus_one(1, 0)
        minus_one(1, 1)
        copy_out(4)
        elu_pass(1, 0)
        exps(2, 0)
        turn(5)
        elu_pass(1, 1)
        exps(2, 1)
        quant_m(0)
        first_matmuls(3, 0)
        gain_pass(1)
        minus_one(2, 0)
        first_matmuls(3, 1)
        minus_one(2, 1)
        second_matmuls(0, 0)
        quant_in(4)
        copy_out(5)
        elu_pass(2, 0)
        second_matmuls(0, 1)
        exps(3, 0)
        elu_pass(2, 1)
        first_matmuls(4, 0)
        dequant(6)
        quant_m(1)
        first_matmuls(4, 1)
        gain_pass(2)
        gate_tanh(0)
        turn(6)
        exps(3, 1)
        gate_pass(0)
        second_matmuls(1, 0)
        minus_one(3, 0)
        quant_in(5)
        second_matmuls(1, 1)
        residual_pass(0)
        minus_one(3, 1)
        elu_pass(3, 0)
        exps(4, 0)
        skip_matmuls(1)
        elu_pass(3, 1)
        gate_tanh(1)
        first_matmuls(5, 0)
        quant_m(2)
        exps(4, 1)
        first_matmuls(5, 1)
        gain_pass(3)
        exps(5, 0)
        second_matmuls(2, 0)
        minus_one(4, 0)
        gate_pass(1)
        copy_out(6)
        elu_pass(4, 0)
        second_matmuls(2, 1)
        minus_one(4, 1)
        quant_in(6)
        residual_pass(1)
        dequant(7)
        first_matmuls(6, 0)
        elu_pass(4, 1)
        skip_matmuls(2)
        gate_tanh(2)
        turn(7)
        quant_m(3)
        exps(5, 1)
        gain_pass(4)
        minus_one(5, 0)
        first_matmuls(6, 1)
        copy_out(7)
        second_matmuls(3, 0)
        gate_pass(2)
        minus_one(5, 1)
        skip_matmuls(6)
        quant_in(7)
        elu_pass(5, 0)
        second_matmuls(3, 1)
        squares(0)
        elu_pass(5, 1)
        first_matmuls(7, 0)
        exps(6, 0)
        scale_up(0)
        residual_pass(2)
        first_matmuls(7, 1)
        gate_tanh(3)
        quant_m(4)
        skip_matmuls(3)
        exps(6, 1)
        gain_pass(5)
        second_matmuls(4, 0)
        minus_one(6, 0)
        minus_one(6, 1)
        gate_pass(3)
        squares(1)
        elu_pass(6, 0)
        second_matmuls(4, 1)
        exps(7, 1)
        scale_up(1)
        elu_pass(6, 1)
        exps(7, 0)
        residual_pass(3)
        gate_tanh(4)
        quant_m(5)
        skip_matmuls(4)
        gain_pass(6)
        minus_one(7, 1)
        second_matmuls(5, 0)
        squares(2)
        gate_pass(4)
        minus_one(7, 0)
        scale_up(2)
        elu_pass(7, 1)
        second_matmuls(5, 1)
        gate_tanh(5)
        elu_pass(7, 0)
        squares(3)
        residual_pass(4)
        norm_pass(0)
        scale_up(3)
        quant_m(6)
        skip_matmuls(5)
        squares(4)
        gain_pass(7)
        second_matmuls(6, 0)
        norm_pass(1)
        scale_up(4)
        second_matmuls(6, 1)
        gate_pass(5)
        norm_pass(3)
        quant_m(7)
        gate_tanh(6)
        residual_pass(5)
        second_matmuls(7, 0)
        second_matmuls(7, 1)
        gate_pass(6)
        squares(5)
        skip_matmuls(7)
        gate_tanh(7)
        residual_pass(6)
        scale_up(5)
        gate_pass(7)
        squares(6)
        norm_pass(5)
        residual_pass(7)
        scale_up(6)
        norm_pass(2)
        squares(7)
        norm_pass(4)
        norm_pass(6)
        scale_up(7)
        norm_pass(7)
